import numpy as np
import ml_dtypes


def mxq(x, axis, fmt="e4m3"):
    dtype, down = {"e4m3": (ml_dtypes.float8_e4m3fn, 7), "e5m2": (ml_dtypes.float8_e5m2, 14)}[fmt]
    v = np.moveaxis(np.asarray(x, np.float32).astype(ml_dtypes.bfloat16).astype(np.float64), axis, -1)
    blocks = v.reshape(v.shape[:-1] + (-1, 32))
    amax = np.abs(blocks).max(-1, keepdims=True)
    byte = np.maximum(np.where(amax > 0, np.frexp(amax)[1] - 1 + 127, 0) - down, 1)
    scale = np.exp2(byte - 127.0)
    codes = (blocks / scale).astype(np.float32).astype(dtype).astype(np.float64)
    return np.moveaxis((codes * scale).reshape(v.shape), -1, axis)


WIDE = False


def mx_kscale(k):
    if not WIDE:
        return np.ones(k)
    levels = np.array([30, -30])
    if k % 512:
        return np.exp2(np.random.permutation(np.resize(levels, k // 32))).repeat(32)
    a = np.empty((k // 512, 16))
    for p in range(k // 512):
        a[p, :8] = np.random.permutation(np.resize(levels, 8))
        for g in range(8):
            far = levels[np.abs(levels - a[p, g]) >= 10]
            a[p, g + 8] = far[np.random.randint(len(far))]
    return np.exp2(a.ravel()).repeat(32)


def f64(x):
    return np.asarray(x).astype(np.float64)


def striped(idx):
    return np.tile(np.asarray(idx).reshape(-1, 16).T, (8, 1)).astype(np.uint16)


def unstriped(offs):
    return offs[:16].T.reshape(-1).astype(np.int64)


E2M1 = np.array([0.0, 0.5, 1.0, 1.5, 2.0, 3.0, 4.0, 6.0, -0.0, -0.5, -1.0, -1.5, -2.0, -3.0, -4.0, -6.0])


def pack_weight(w, fmt):
    k, n = w.shape
    w = f64(np.asarray(w, np.float32).astype(ml_dtypes.bfloat16)).reshape(k // 32, 32, n)
    amax = np.abs(w).max(1)
    if fmt in ("e4m3", "e5m2"):
        byte = np.frexp(amax)[1] - 1 + 127 - (7 if fmt == "e4m3" else 14)
    else:
        mant, ex = np.frexp(amax / 6.0)
        byte = np.where(mant > 0.5, ex, ex - 1) + 127
    byte = np.clip(np.where(amax > 0, byte, 1), 1, 254)
    scaled = (w * np.exp2(127.0 - byte)[:, None, :]).reshape(k, n).astype(np.float32)
    by_word = np.ascontiguousarray(scaled.reshape(k // 512, 128, 4, n).transpose(0, 1, 3, 2))
    if fmt in ("e4m3", "e5m2"):
        words = by_word.astype(ml_dtypes.float8_e4m3fn if fmt == "e4m3" else ml_dtypes.float8_e5m2).view(np.uint8)
    else:
        c = by_word.astype(ml_dtypes.float4_e2m1fn).view(np.uint8) & 0xF
        words = (c[..., 0::2] | (c[..., 1::2] << 4)).reshape(k // 512, 128, 2 * n)
    return np.ascontiguousarray(words), np.ascontiguousarray(byte.astype(np.uint8).reshape(k // 512, 16, n))


def unpack_weight(words, scales, fmt):
    g, _, n = scales.shape
    words = np.ascontiguousarray(words).reshape(g, 128, n, -1)
    if fmt in ("e4m3", "e5m2"):
        vals = words.view(ml_dtypes.float8_e4m3fn if fmt == "e4m3" else ml_dtypes.float8_e5m2).astype(np.float64)
    else:
        nib = np.empty((g, 128, n, 4), np.uint8)
        nib[..., 0::2] = words & 0xF
        nib[..., 1::2] = words >> 4
        vals = E2M1[nib]
    vals = vals * np.repeat(np.exp2(scales.astype(np.float64) - 127.0), 8, axis=1)[..., None]
    return vals.transpose(0, 1, 3, 2).reshape(g * 512, n)


def sigmoid(v):
    return 1.0 / (1.0 + np.exp(-v))


K, T, J, R, O, N, L, E = 512, 1024, 256, 512, 128, 256, 512, 1024


def setup_inputs():
    n = np.random.standard_normal
    idx = np.random.permutation(T)[:J]
    idx2 = np.random.permutation(J)[:O]
    idx3 = np.random.permutation(J)[:O]
    idx4 = np.random.permutation(E)[:O]
    fk = mx_kscale(K)
    fr = mx_kscale(R)
    fl = mx_kscale(L)
    xtp = pack_weight(n((K, T)) / fk[:, None], "e4m3")
    wp = pack_weight(n((K, R)) * 1 / np.sqrt(K) * fk[:, None], "e2m1")
    w2p = pack_weight(n((K, R)) * 1 / np.sqrt(K) * fk[:, None] * fr, "e5m2")
    wbp = pack_weight(n((R, N)) * 1 / np.sqrt(R) / fr[:, None], "e5m2")
    sxp = pack_weight(n((L, O)) / fl[:, None], "e2m1")
    wsp = pack_weight(n((L, N)) * 1 / np.sqrt(L) * fl[:, None], "e5m2")
    return {
        "xt_words": xtp[0],
        "xt_scales": xtp[1],
        "w_words": wp[0],
        "w_scales": wp[1],
        "w2_words": w2p[0],
        "w2_scales": w2p[1],
        "sg": (np.random.uniform(0.6, 1.6, (R, 1))).astype(np.float32),
        "wb_words": wbp[0],
        "wb_scales": wbp[1],
        "sx_words": sxp[0],
        "sx_scales": sxp[1],
        "ws_words": wsp[0],
        "ws_scales": wsp[1],
        "offs": striped(idx),
        "offs2": striped(idx2),
        "offs3": striped(idx3),
        "offs4": striped(idx4),
    }


def reference(xt_words, xt_scales, w_words, w_scales, w2_words, w2_scales, sg, wb_words, wb_scales, sx_words, sx_scales, ws_words, ws_scales, offs, offs2, offs3, offs4):
    idx = unstriped(offs)
    idx2 = unstriped(offs2)
    idx3 = unstriped(offs3)
    idx4 = unstriped(offs4)
    xtu = unpack_weight(xt_words, xt_scales, "e4m3")
    wu = unpack_weight(w_words, w_scales, "e2m1")
    w2u = unpack_weight(w2_words, w2_scales, "e5m2")
    wbu = unpack_weight(wb_words, wb_scales, "e5m2")
    sxu = unpack_weight(sx_words, sx_scales, "e2m1")
    wsu = unpack_weight(ws_words, ws_scales, "e5m2")
    xtidxg = xtu[:, idx]
    a = wu.T @ xtidxg
    b = w2u.T @ xtidxg
    hid = np.maximum(b[:, idx2], b[:, idx3]) * sigmoid(a[:, idx3] * f64(sg))
    hidq = mxq(hid, 0, "e4m3")
    p = wbu.T @ hidq + wsu.T @ sxu
    y = np.zeros((N, E))
    y[:, idx4] = p
    return y

@@ -1,0 +1,197 @@
+from contextlib import ExitStack
+
+import concourse.mybir as mybir
+
+K, T, J, R, O, N, L, E = 512, 1024, 256, 512, 128, 256, 512, 1024
+FLOPS = 2 * (2 * K * R * J + R * N * O + L * N * O)
+
+F32 = mybir.dt.float32
+BF16 = mybir.dt.bfloat16
+I32 = mybir.dt.int32
+U32 = mybir.dt.uint32
+U16 = mybir.dt.uint16
+U8 = mybir.dt.uint8
+E4M3 = mybir.dt.float8_e4m3fn_x4
+E5M2 = mybir.dt.float8_e5m2_x4
+E2M1 = mybir.dt.float4_e2m1fn_x4
+ACT = mybir.ActivationFunctionType
+ALU = mybir.AluOpType
+
+P = 128
+PACK = 4
+
+
+def words_i32(words):
+    return words[0].rearrange("p n t -> p (n t)").bitcast(I32)
+
+
+def tile_list_twow_agree_skip_scattered_kernel(
+    tc, xt_words, xt_scales, w_words, w_scales, w2_words, w2_scales, sg, wb_words, wb_scales,
+    sx_words, sx_scales, ws_words, ws_scales, offs, offs2, offs3, offs4, out,
+):
+    nc = tc.nc
+    with ExitStack() as ctx:
+        sb = ctx.enter_context(tc.tile_pool(name="sb", bufs=1))
+        psum = ctx.enter_context(tc.psum_pool(name="psum", bufs=8))
+
+        def new(shape, dtype, name, tag=None):
+            return sb.tile(shape, dtype, name=name, tag=tag or name, align_bytes=64)
+
+        idx = new([P, J // 16], U16, "idx")
+        idx2 = new([P, O // 16], U16, "idx2")
+        idx3 = new([P, O // 16], U16, "idx3")
+        idx4 = new([P, O // 16], U16, "idx4")
+        xt_w = new([P, T], I32, "xt_w")
+        xt_s = new([P, T], U8, "xt_s")
+        raw_s = new([P, 2 * R], U8, "raw_s")
+        dealt_s = new([P, 2 * R], U8, "dealt_s")
+        w2_raw = new([P, R], I32, "w2_raw")
+        w_raw = new([P, R // 2], I32, "w_raw")
+        w2_w = new([P, R], U32, "w2_w")
+        w_w = new([P, R], U16, "w_w")
+        slope = new([P, PACK], F32, "slope")
+        xg_s = new([P, J], U8, "xg_s")
+        pages = [new([P, E], F32, "page%d" % h) for h in range(2)]
+
+        def load_plane(dst, src):
+            for q in range(4):
+                nc.sync.dma_start(out=dst[32 * q : 32 * q + 4, :], in_=src[4 * q : 4 * q + 4, :])
+
+        nc.vector.memset(raw_s[:].bitcast(I32), 0)
+        nc.vector.memset(xt_s[:].bitcast(I32), 0)
+        nc.sync.dma_start(idx[:], offs)
+        nc.sync.dma_start(out=raw_s[0:16, 0:R].bitcast(I32), in_=w2_scales[0].bitcast(I32))
+        nc.scalar.dma_start(out=raw_s[0:16, R : 2 * R].bitcast(I32), in_=w_scales[0].bitcast(I32))
+        nc.scalar.dma_start(out=xt_w[:], in_=words_i32(xt_words))
+        load_plane(xt_s[:].bitcast(I32), xt_scales[0].bitcast(I32))
+        nc.sync.dma_start(out=w2_raw[:], in_=words_i32(w2_words))
+        nc.sync.dma_start(out=w_raw[:], in_=w_words[0].bitcast(I32))
+        nc.sync.dma_start(idx2[:], offs2)
+        nc.sync.dma_start(idx3[:], offs3)
+        nc.sync.dma_start(out=slope[:], in_=sg.rearrange("(p t) o -> p (t o)", t=PACK))
+        nc.sync.dma_start(idx4[:], offs4)
+
+        warm = new([P, 2], F32, "warm")
+        nc.vector.memset(warm[:, 0:1], 0.0)
+        nc.scalar.activation(out=warm[:, 1:2], in_=warm[:, 0:1], func=ACT.Sigmoid)
+        for page in pages:
+            nc.vector.memset(page[:], 0.0)
+
+        nc.vector.tensor_copy(
+            out=dealt_s[:].rearrange("p (x t c i) -> p x c t i", x=2, t=PACK, i=16),
+            in_=raw_s[:].rearrange("p (x c i t) -> p x c t i", x=2, t=PACK, i=16),
+        )
+        for q in range(1, 4):
+            nc.scalar.dma_start(out=dealt_s[32 * q : 32 * q + 4, :].bitcast(I32), in_=dealt_s[4 * q : 4 * q + 4, :].bitcast(I32))
+
+        nc.vector.tensor_copy(xg_s[:], xt_s[:].indirect(idx[:]))
+        xg_w = new([P, J], U32, "xg_w", tag="raw_s")
+        nc.vector.tensor_copy(xg_w[:], xt_w[:].bitcast(U32).indirect(idx[:]))
+        nc.scalar.copy(
+            out=w2_w[:].rearrange("p (t c i) -> p c t i", t=PACK, i=4),
+            in_=w2_raw[:].bitcast(U32).rearrange("p (c i t) -> p c t i", t=PACK, i=4),
+        )
+        nc.vector.tensor_copy(
+            out=w_w[:].rearrange("p (t c i) -> p c t i", t=PACK, i=8),
+            in_=w_raw[:].bitcast(U16).rearrange("p (c i t) -> p c t i", t=PACK, i=8),
+        )
+
+        late_s = new([P, N + N + O], U8, "late_s", tag="xt_s")
+        late_w = new([P, 2 * N], I32, "late_w", tag="w2_raw")
+        sx_w = new([P, O // 2], I32, "sx_w", tag="w_raw")
+        ws_w = late_w[:, 0:N]
+        wb_w = late_w[:, N : 2 * N]
+        nc.gpsimd.memset(late_s[:].bitcast(I32), 0)
+        nc.sync.dma_start(out=ws_w, in_=words_i32(ws_words))
+        nc.sync.dma_start(out=sx_w[:], in_=sx_words[0].bitcast(I32))
+        nc.sync.dma_start(out=wb_w, in_=words_i32(wb_words))
+        load_plane(late_s[:, 0:N].bitcast(I32), ws_scales[0].bitcast(I32))
+        load_plane(late_s[:, 2 * N : 2 * N + O].bitcast(I32), sx_scales[0].bitcast(I32))
+        load_plane(late_s[:, N : 2 * N].bitcast(I32), wb_scales[0].bitcast(I32))
+
+        b2 = new([P, PACK, O], F32, "b2")
+        b3 = new([P, PACK, O], F32, "b3")
+        gate = new([P, PACK, O], F32, "gate")
+        top = new([P, PACK, O], F32, "top")
+        a_rows = [new([P, J], F32, "a%d_rows" % t) for t in range(PACK)]
+        b_rows = [new([P, J], F32, "b%d_rows" % t) for t in range(PACK)]
+
+        def second_matrix(t):
+            cols = slice(P * t, P * (t + 1))
+            b_ps = psum.tile([P, J], F32, name="acc")
+            nc.tensor.matmul_mx(
+                out=b_ps[:], lhsT=w2_w[:, cols].bitcast(E5M2), lhsT_scale=dealt_s[:, cols],
+                rhs=xg_w[:].bitcast(E4M3), rhs_scale=xg_s[:], start=True, stop=True,
+            )
+            if t == 0:
+                nc.vector.tensor_copy(out=b_rows[t][:], in_=b_ps[:])
+            else:
+                nc.scalar.copy(out=b_rows[t][:], in_=b_ps[:])
+
+        def first_matrix(t):
+            cols = slice(P * t, P * (t + 1))
+            a_ps = psum.tile([P, J], F32, name="acc")
+            nc.tensor.matmul_mx(
+                out=a_ps[:], lhsT=w_w[:, cols].bitcast(E2M1), lhsT_scale=dealt_s[:, R + P * t : R + P * (t + 1)],
+                rhs=xg_w[:].bitcast(E4M3), rhs_scale=xg_s[:], start=True, stop=True,
+            )
+            nc.scalar.copy(out=a_rows[t][:], in_=a_ps[:])
+
+        def look_up_gate(t):
+            nc.scalar.activation(out=gate[:, t, :], in_=a_rows[t][:].indirect(idx3[:]), func=ACT.Sigmoid, scale=slope[:, t : t + 1])
+
+        second_matrix(0)
+        second_matrix(1)
+        first_matrix(0)
+        second_matrix(2)
+        look_up_gate(0)
+        first_matrix(1)
+        second_matrix(3)
+        look_up_gate(1)
+        first_matrix(2)
+        first_matrix(3)
+        look_up_gate(2)
+        look_up_gate(3)
+        for t in range(PACK):
+            nc.vector.tensor_copy(b2[:, t, :], b_rows[t][:].indirect(idx2[:]))
+            nc.vector.tensor_copy(b3[:, t, :], b_rows[t][:].indirect(idx3[:]))
+        nc.vector.tensor_tensor(out=top[:, 0:3, :], in0=b2[:, 0:3, :], in1=b3[:, 0:3, :], op=ALU.max)
+        nc.vector.tensor_tensor(out=top[:, 3, :], in0=b2[:, 3, :], in1=b3[:, 3, :], op=ALU.max)
+
+        hid = new([P, O * PACK], BF16, "hid")
+        hid_w = new([P, O], U32, "hid_w")
+        hid_s = new([P, O], U8, "hid_s")
+        halves = [slice(0, O // 2), slice(O // 2, O)]
+        for half in halves:
+            nc.vector.tensor_tensor(
+                out=hid[:, PACK * half.start : PACK * half.stop].rearrange("p (c i t) -> p c t i", t=PACK, i=4),
+                in0=top[:, :, half].rearrange("p t (c i) -> p c t i", i=4),
+                in1=gate[:, :, half].rearrange("p t (c i) -> p c t i", i=4),
+                op=ALU.mult,
+            )
+        for half in halves:
+            nc.vector.quantize_mx(out=hid_w[:, half].bitcast(E4M3), scales=hid_s[:, half], in_=hid[:, PACK * half.start : PACK * half.stop])
+
+        sums = []
+        for h in range(2):
+            cols = slice(P * h, P * (h + 1))
+            p_ps = psum.tile([P, J], F32, name="acc")
+            nc.tensor.matmul_mx(
+                out=p_ps[:, 0:O], lhsT=ws_w[:, cols].bitcast(E5M2), lhsT_scale=late_s[:, cols],
+                rhs=sx_w[:].bitcast(E2M1), rhs_scale=late_s[:, 2 * N : 2 * N + O], start=True, stop=False,
+            )
+            sums.append(p_ps)
+        for h in range(2):
+            cols = slice(P * h, P * (h + 1))
+            nc.tensor.matmul_mx(
+                out=sums[h][:, 0:O], lhsT=wb_w[:, cols].bitcast(E5M2), lhsT_scale=late_s[:, N + P * h : N + P * (h + 1)],
+                rhs=hid_w[:].bitcast(E4M3), rhs_scale=hid_s[:], start=False, stop=True,
+            )
+        p0 = new([P, O], F32, "p0")
+        p1 = new([P, O], F32, "p1")
+        nc.vector.tensor_copy(out=p0[:], in_=sums[0][:, 0:O])
+        nc.vector.tensor_copy(pages[0][:].indirect(idx4[:]), p0[:])
+        nc.sync.dma_start(out=out[0:P, :], in_=pages[0][:])
+        nc.scalar.copy(out=p1[:], in_=sums[1][:, 0:O])
+        nc.scalar.activation(out=pages[1][:].indirect(idx4[:]), in_=p1[:], func=ACT.Copy)
+        nc.scalar.dma_start(out=out[P : 2 * P, :], in_=pages[1][:])

@@ -44,6 +44,7 @@ def tile_list_twow_agree_skip_scattered_kernel(
         xt_w = new([P, T], I32, "xt_w")
         xt_s = new([P, T], U8, "xt_s")
         raw_s = new([P, 2 * R], U8, "raw_s")
+        staged_s = new([16, 2 * R // 4], I32, "staged_s")
         dealt_s = new([P, 2 * R], U8, "dealt_s")
         w2_raw = new([P, R], I32, "w2_raw")
         w_raw = new([P, R // 2], I32, "w_raw")
@@ -58,12 +59,14 @@ def tile_list_twow_agree_skip_scattered_kernel(
                 nc.sync.dma_start(out=dst[32 * q : 32 * q + 4, :], in_=src[4 * q : 4 * q + 4, :])
 
         nc.vector.memset(raw_s[:].bitcast(I32), 0)
-        nc.vector.memset(xt_s[:].bitcast(I32), 0)
+        nc.gpsimd.memset(xt_s[:].bitcast(I32), 0)
         nc.sync.dma_start(idx[:], offs)
-        nc.sync.dma_start(out=raw_s[0:16, 0:R].bitcast(I32), in_=w2_scales[0].bitcast(I32))
-        nc.scalar.dma_start(out=raw_s[0:16, R : 2 * R].bitcast(I32), in_=w_scales[0].bitcast(I32))
-        nc.scalar.dma_start(out=xt_w[:], in_=words_i32(xt_words))
-        load_plane(xt_s[:].bitcast(I32), xt_scales[0].bitcast(I32))
+        nc.sync.dma_start(out=staged_s[:, 0 : R // 4], in_=w2_scales[0].bitcast(I32))
+        nc.scalar.dma_start(out=staged_s[:, R // 4 : R // 2], in_=w_scales[0].bitcast(I32))
+        for q in range(4):
+            queue = nc.sync if q < 2 else nc.scalar
+            queue.dma_start(out=xt_s[32 * q : 32 * q + 4, :].bitcast(I32), in_=xt_scales[0][4 * q : 4 * q + 4, :].bitcast(I32))
+        nc.sync.dma_start(out=xt_w[:], in_=words_i32(xt_words))
         nc.sync.dma_start(out=w2_raw[:], in_=words_i32(w2_words))
         nc.sync.dma_start(out=w_raw[:], in_=w_words[0].bitcast(I32))
         nc.sync.dma_start(idx2[:], offs2)
@@ -77,24 +80,24 @@ def tile_list_twow_agree_skip_scattered_kernel(
         for page in pages:
             nc.vector.memset(page[:], 0.0)
 
-        nc.vector.tensor_copy(
-            out=dealt_s[:].rearrange("p (x t c i) -> p x c t i", x=2, t=PACK, i=16),
-            in_=raw_s[:].rearrange("p (x c i t) -> p x c t i", x=2, t=PACK, i=16),
-        )
-        for q in range(1, 4):
-            nc.scalar.dma_start(out=dealt_s[32 * q : 32 * q + 4, :].bitcast(I32), in_=dealt_s[4 * q : 4 * q + 4, :].bitcast(I32))
+        for q in range(4):
+            nc.scalar.dma_start(out=raw_s[32 * q : 32 * q + 4, :].bitcast(I32), in_=staged_s[4 * q : 4 * q + 4, :])
 
         nc.vector.tensor_copy(xg_s[:], xt_s[:].indirect(idx[:]))
-        xg_w = new([P, J], U32, "xg_w", tag="raw_s")
+        xg_w = new([P, J], U32, "xg_w")
         nc.vector.tensor_copy(xg_w[:], xt_w[:].bitcast(U32).indirect(idx[:]))
-        nc.scalar.copy(
-            out=w2_w[:].rearrange("p (t c i) -> p c t i", t=PACK, i=4),
-            in_=w2_raw[:].bitcast(U32).rearrange("p (c i t) -> p c t i", t=PACK, i=4),
-        )
-        nc.vector.tensor_copy(
-            out=w_w[:].rearrange("p (t c i) -> p c t i", t=PACK, i=8),
-            in_=w_raw[:].bitcast(U16).rearrange("p (c i t) -> p c t i", t=PACK, i=8),
-        )
+
+        def deal(copy, dst, src, run):
+            for u in range(2):
+                copy(
+                    out=dst.rearrange("p (u t c i) -> p u c t i", u=2, t=2, i=run)[:, u],
+                    in_=src.rearrange("p (c i u t) -> p u c t i", u=2, t=2, i=run)[:, u],
+                )
+
+        deal(nc.scalar.copy, w2_w[:], w2_raw[:].bitcast(U32), 4)
+        deal(nc.vector.tensor_copy, dealt_s[:, 0:R], raw_s[:, 0:R], 16)
+        deal(nc.scalar.copy, w_w[:], w_raw[:].bitcast(U16), 8)
+        deal(nc.vector.tensor_copy, dealt_s[:, R : 2 * R], raw_s[:, R : 2 * R], 16)
 
         late_s = new([P, N + N + O], U8, "late_s", tag="xt_s")
         late_w = new([P, 2 * N], I32, "late_w", tag="w2_raw")

@@ -126,10 +126,7 @@ def tile_list_twow_agree_skip_scattered_kernel(
                 out=b_ps[:], lhsT=w2_w[:, cols].bitcast(E5M2), lhsT_scale=dealt_s[:, cols],
                 rhs=xg_w[:].bitcast(E4M3), rhs_scale=xg_s[:], start=True, stop=True,
             )
-            if t == 0:
-                nc.vector.tensor_copy(out=b_rows[t][:], in_=b_ps[:])
-            else:
-                nc.scalar.copy(out=b_rows[t][:], in_=b_ps[:])
+            nc.scalar.copy(out=b_rows[t][:], in_=b_ps[:])
 
         def first_matrix(t):
             cols = slice(P * t, P * (t + 1))
@@ -145,33 +142,35 @@ def tile_list_twow_agree_skip_scattered_kernel(
 
         second_matrix(0)
         second_matrix(1)
-        first_matrix(0)
         second_matrix(2)
-        look_up_gate(0)
-        first_matrix(1)
+        first_matrix(0)
         second_matrix(3)
-        look_up_gate(1)
-        first_matrix(2)
-        first_matrix(3)
-        look_up_gate(2)
-        look_up_gate(3)
+        for t in range(PACK):
+            if t + 1 < PACK:
+                first_matrix(t + 1)
+            look_up_gate(t)
         for t in range(PACK):
             nc.vector.tensor_copy(b2[:, t, :], b_rows[t][:].indirect(idx2[:]))
             nc.vector.tensor_copy(b3[:, t, :], b_rows[t][:].indirect(idx3[:]))
-        nc.vector.tensor_tensor(out=top[:, 0:3, :], in0=b2[:, 0:3, :], in1=b3[:, 0:3, :], op=ALU.max)
-        nc.vector.tensor_tensor(out=top[:, 3, :], in0=b2[:, 3, :], in1=b3[:, 3, :], op=ALU.max)
+        for pair in (slice(0, 2), slice(2, 4)):
+            nc.vector.tensor_tensor(out=top[:, pair, :], in0=b2[:, pair, :], in1=b3[:, pair, :], op=ALU.max)
 
         hid = new([P, O * PACK], BF16, "hid")
         hid_w = new([P, O], U32, "hid_w")
         hid_s = new([P, O], U8, "hid_s")
         halves = [slice(0, O // 2), slice(O // 2, O)]
-        for half in halves:
+
+        def gated(pair, places):
             nc.vector.tensor_tensor(
-                out=hid[:, PACK * half.start : PACK * half.stop].rearrange("p (c i t) -> p c t i", t=PACK, i=4),
-                in0=top[:, :, half].rearrange("p t (c i) -> p c t i", i=4),
-                in1=gate[:, :, half].rearrange("p t (c i) -> p c t i", i=4),
+                out=hid[:, PACK * places.start : PACK * places.stop].rearrange("p (c i t) -> p c t i", t=PACK, i=4)[:, :, pair, :],
+                in0=top[:, pair, places].rearrange("p t (c i) -> p c t i", i=4),
+                in1=gate[:, pair, places].rearrange("p t (c i) -> p c t i", i=4),
                 op=ALU.mult,
             )
+
+        gated(slice(0, 2), slice(0, O))
+        for half in halves:
+            gated(slice(2, 4), half)
         for half in halves:
             nc.vector.quantize_mx(out=hid_w[:, half].bitcast(E4M3), scales=hid_s[:, half], in_=hid[:, PACK * half.start : PACK * half.stop])
 

@@ -58,8 +58,8 @@ def tile_list_twow_agree_skip_scattered_kernel(
             for q in range(4):
                 nc.sync.dma_start(out=dst[32 * q : 32 * q + 4, :], in_=src[4 * q : 4 * q + 4, :])
 
+        nc.vector.memset(xt_s[:].bitcast(I32), 0)
         nc.vector.memset(raw_s[:].bitcast(I32), 0)
-        nc.gpsimd.memset(xt_s[:].bitcast(I32), 0)
         nc.sync.dma_start(idx[:], offs)
         nc.sync.dma_start(out=staged_s[:, 0 : R // 4], in_=w2_scales[0].bitcast(I32))
         nc.scalar.dma_start(out=staged_s[:, R // 4 : R // 2], in_=w_scales[0].bitcast(I32))
@@ -87,17 +87,17 @@ def tile_list_twow_agree_skip_scattered_kernel(
         xg_w = new([P, J], U32, "xg_w")
         nc.vector.tensor_copy(xg_w[:], xt_w[:].bitcast(U32).indirect(idx[:]))
 
-        def deal(copy, dst, src, run):
-            for u in range(2):
+        def deal(copy, dst, src, run, pieces):
+            for u in range(pieces):
                 copy(
-                    out=dst.rearrange("p (u t c i) -> p u c t i", u=2, t=2, i=run)[:, u],
-                    in_=src.rearrange("p (c i u t) -> p u c t i", u=2, t=2, i=run)[:, u],
+                    out=dst.rearrange("p (u t c i) -> p u c t i", u=pieces, t=PACK // pieces, i=run)[:, u],
+                    in_=src.rearrange("p (c i u t) -> p u c t i", u=pieces, t=PACK // pieces, i=run)[:, u],
                 )
 
-        deal(nc.scalar.copy, w2_w[:], w2_raw[:].bitcast(U32), 4)
-        deal(nc.vector.tensor_copy, dealt_s[:, 0:R], raw_s[:, 0:R], 16)
-        deal(nc.scalar.copy, w_w[:], w_raw[:].bitcast(U16), 8)
-        deal(nc.vector.tensor_copy, dealt_s[:, R : 2 * R], raw_s[:, R : 2 * R], 16)
+        deal(nc.scalar.copy, w2_w[:], w2_raw[:].bitcast(U32), 4, 2)
+        deal(nc.vector.tensor_copy, dealt_s[:, 0:R], raw_s[:, 0:R], 16, 4)
+        deal(nc.scalar.copy, w_w[:], w_raw[:].bitcast(U16), 8, 2)
+        deal(nc.vector.tensor_copy, dealt_s[:, R : 2 * R], raw_s[:, R : 2 * R], 16, 2)
 
         late_s = new([P, N + N + O], U8, "late_s", tag="xt_s")
         late_w = new([P, 2 * N], I32, "late_w", tag="w2_raw")

from contextlib import ExitStack

import concourse.mybir as mybir

K, T, J, R, O, N, L, E = 512, 1024, 256, 512, 128, 256, 512, 1024
FLOPS = 2 * (2 * K * R * J + R * N * O + L * N * O)

F32 = mybir.dt.float32
BF16 = mybir.dt.bfloat16
I32 = mybir.dt.int32
U32 = mybir.dt.uint32
U16 = mybir.dt.uint16
U8 = mybir.dt.uint8
E4M3 = mybir.dt.float8_e4m3fn_x4
E5M2 = mybir.dt.float8_e5m2_x4
E2M1 = mybir.dt.float4_e2m1fn_x4
ACT = mybir.ActivationFunctionType
ALU = mybir.AluOpType

P = 128
PACK = 4


def words_i32(words):
    return words[0].rearrange("p n t -> p (n t)").bitcast(I32)


def tile_list_twow_agree_skip_scattered_kernel(
    tc, xt_words, xt_scales, w_words, w_scales, w2_words, w2_scales, sg, wb_words, wb_scales,
    sx_words, sx_scales, ws_words, ws_scales, offs, offs2, offs3, offs4, out,
):
    nc = tc.nc
    with ExitStack() as ctx:
        sb = ctx.enter_context(tc.tile_pool(name="sb", bufs=1))
        psum = ctx.enter_context(tc.psum_pool(name="psum", bufs=8))

        def new(shape, dtype, name, tag=None):
            return sb.tile(shape, dtype, name=name, tag=tag or name, align_bytes=64)

        idx = new([P, J // 16], U16, "idx")
        idx2 = new([P, O // 16], U16, "idx2")
        idx3 = new([P, O // 16], U16, "idx3")
        idx4 = new([P, O // 16], U16, "idx4")
        xt_w = new([P, T], I32, "xt_w")
        xt_s = new([P, T], U8, "xt_s")
        raw_s = new([P, 2 * R], U8, "raw_s")
        staged_s = new([16, 2 * R // 4], I32, "staged_s")
        dealt_s = new([P, 2 * R], U8, "dealt_s")
        w2_raw = new([P, R], I32, "w2_raw")
        w_raw = new([P, R // 2], I32, "w_raw")
        w2_w = new([P, R], U32, "w2_w")
        w_w = new([P, R], U16, "w_w")
        slope = new([P, PACK], F32, "slope")
        xg_s = new([P, J], U8, "xg_s")
        pages = [new([P, E], F32, "page%d" % h) for h in range(2)]

        def load_plane(dst, src):
            for q in range(4):
                nc.sync.dma_start(out=dst[32 * q : 32 * q + 4, :], in_=src[4 * q : 4 * q + 4, :])

        nc.vector.memset(xt_s[:].bitcast(I32), 0)
        nc.vector.memset(raw_s[:].bitcast(I32), 0)
        nc.sync.dma_start(idx[:], offs)
        nc.sync.dma_start(out=staged_s[:, 0 : R // 4], in_=w2_scales[0].bitcast(I32))
        nc.scalar.dma_start(out=staged_s[:, R // 4 : R // 2], in_=w_scales[0].bitcast(I32))
        for q in range(4):
            queue = nc.sync if q < 2 else nc.scalar
            queue.dma_start(out=xt_s[32 * q : 32 * q + 4, :].bitcast(I32), in_=xt_scales[0][4 * q : 4 * q + 4, :].bitcast(I32))
        nc.sync.dma_start(out=xt_w[:], in_=words_i32(xt_words))
        nc.sync.dma_start(out=w2_raw[:], in_=words_i32(w2_words))
        nc.sync.dma_start(out=w_raw[:], in_=w_words[0].bitcast(I32))
        nc.sync.dma_start(idx2[:], offs2)
        nc.sync.dma_start(idx3[:], offs3)
        nc.sync.dma_start(out=slope[:], in_=sg.rearrange("(p t) o -> p (t o)", t=PACK))
        nc.sync.dma_start(idx4[:], offs4)

        warm = new([P, 2], F32, "warm")
        nc.vector.memset(warm[:, 0:1], 0.0)
        nc.scalar.activation(out=warm[:, 1:2], in_=warm[:, 0:1], func=ACT.Sigmoid)
        for page in pages:
            nc.vector.memset(page[:], 0.0)

        for q in range(4):
            nc.scalar.dma_start(out=raw_s[32 * q : 32 * q + 4, :].bitcast(I32), in_=staged_s[4 * q : 4 * q + 4, :])

        nc.vector.tensor_copy(xg_s[:], xt_s[:].indirect(idx[:]))
        xg_w = new([P, J], U32, "xg_w")
        nc.vector.tensor_copy(xg_w[:], xt_w[:].bitcast(U32).indirect(idx[:]))

        def deal(copy, dst, src, run, pieces):
            for u in range(pieces):
                copy(
                    out=dst.rearrange("p (u t c i) -> p u c t i", u=pieces, t=PACK // pieces, i=run)[:, u],
                    in_=src.rearrange("p (c i u t) -> p u c t i", u=pieces, t=PACK // pieces, i=run)[:, u],
                )

        deal(nc.scalar.copy, w2_w[:], w2_raw[:].bitcast(U32), 4, 2)
        deal(nc.vector.tensor_copy, dealt_s[:, 0:R], raw_s[:, 0:R], 16, 4)
        deal(nc.scalar.copy, w_w[:], w_raw[:].bitcast(U16), 8, 2)
        deal(nc.vector.tensor_copy, dealt_s[:, R : 2 * R], raw_s[:, R : 2 * R], 16, 2)

        late_s = new([P, N + N + O], U8, "late_s", tag="xt_s")
        late_w = new([P, 2 * N], I32, "late_w", tag="w2_raw")
        sx_w = new([P, O // 2], I32, "sx_w", tag="w_raw")
        ws_w = late_w[:, 0:N]
        wb_w = late_w[:, N : 2 * N]
        nc.gpsimd.memset(late_s[:].bitcast(I32), 0)
        nc.sync.dma_start(out=ws_w, in_=words_i32(ws_words))
        nc.sync.dma_start(out=sx_w[:], in_=sx_words[0].bitcast(I32))
        nc.sync.dma_start(out=wb_w, in_=words_i32(wb_words))
        load_plane(late_s[:, 0:N].bitcast(I32), ws_scales[0].bitcast(I32))
        load_plane(late_s[:, 2 * N : 2 * N + O].bitcast(I32), sx_scales[0].bitcast(I32))
        load_plane(late_s[:, N : 2 * N].bitcast(I32), wb_scales[0].bitcast(I32))

        b2 = new([P, PACK, O], F32, "b2")
        b3 = new([P, PACK, O], F32, "b3")
        gate = new([P, PACK, O], F32, "gate")
        top = new([P, PACK, O], F32, "top")
        a_rows = [new([P, J], F32, "a%d_rows" % t) for t in range(PACK)]
        b_rows = [new([P, J], F32, "b%d_rows" % t) for t in range(PACK)]

        def second_matrix(t):
            cols = slice(P * t, P * (t + 1))
            b_ps = psum.tile([P, J], F32, name="acc")
            nc.tensor.matmul_mx(
                out=b_ps[:], lhsT=w2_w[:, cols].bitcast(E5M2), lhsT_scale=dealt_s[:, cols],
                rhs=xg_w[:].bitcast(E4M3), rhs_scale=xg_s[:], start=True, stop=True,
            )
            nc.scalar.copy(out=b_rows[t][:], in_=b_ps[:])

        def first_matrix(t):
            cols = slice(P * t, P * (t + 1))
            a_ps = psum.tile([P, J], F32, name="acc")
            nc.tensor.matmul_mx(
                out=a_ps[:], lhsT=w_w[:, cols].bitcast(E2M1), lhsT_scale=dealt_s[:, R + P * t : R + P * (t + 1)],
                rhs=xg_w[:].bitcast(E4M3), rhs_scale=xg_s[:], start=True, stop=True,
            )
            nc.scalar.copy(out=a_rows[t][:], in_=a_ps[:])

        def look_up_gate(t):
            nc.scalar.activation(out=gate[:, t, :], in_=a_rows[t][:].indirect(idx3[:]), func=ACT.Sigmoid, scale=slope[:, t : t + 1])

        second_matrix(0)
        second_matrix(1)
        second_matrix(2)
        first_matrix(0)
        second_matrix(3)
        for t in range(PACK):
            if t + 1 < PACK:
                first_matrix(t + 1)
            look_up_gate(t)
        for t in range(PACK):
            nc.vector.tensor_copy(b2[:, t, :], b_rows[t][:].indirect(idx2[:]))
            nc.vector.tensor_copy(b3[:, t, :], b_rows[t][:].indirect(idx3[:]))
        for pair in (slice(0, 2), slice(2, 4)):
            nc.vector.tensor_tensor(out=top[:, pair, :], in0=b2[:, pair, :], in1=b3[:, pair, :], op=ALU.max)

        hid = new([P, O * PACK], BF16, "hid")
        hid_w = new([P, O], U32, "hid_w")
        hid_s = new([P, O], U8, "hid_s")
        halves = [slice(0, O // 2), slice(O // 2, O)]

        def gated(pair, places):
            nc.vector.tensor_tensor(
                out=hid[:, PACK * places.start : PACK * places.stop].rearrange("p (c i t) -> p c t i", t=PACK, i=4)[:, :, pair, :],
                in0=top[:, pair, places].rearrange("p t (c i) -> p c t i", i=4),
                in1=gate[:, pair, places].rearrange("p t (c i) -> p c t i", i=4),
                op=ALU.mult,
            )

        gated(slice(0, 2), slice(0, O))
        for half in halves:
            gated(slice(2, 4), half)
        for half in halves:
            nc.vector.quantize_mx(out=hid_w[:, half].bitcast(E4M3), scales=hid_s[:, half], in_=hid[:, PACK * half.start : PACK * half.stop])

        sums = []
        for h in range(2):
            cols = slice(P * h, P * (h + 1))
            p_ps = psum.tile([P, J], F32, name="acc")
            nc.tensor.matmul_mx(
                out=p_ps[:, 0:O], lhsT=ws_w[:, cols].bitcast(E5M2), lhsT_scale=late_s[:, cols],
                rhs=sx_w[:].bitcast(E2M1), rhs_scale=late_s[:, 2 * N : 2 * N + O], start=True, stop=False,
            )
            sums.append(p_ps)
        for h in range(2):
            cols = slice(P * h, P * (h + 1))
            nc.tensor.matmul_mx(
                out=sums[h][:, 0:O], lhsT=wb_w[:, cols].bitcast(E5M2), lhsT_scale=late_s[:, N + P * h : N + P * (h + 1)],
                rhs=hid_w[:].bitcast(E4M3), rhs_scale=hid_s[:], start=False, stop=True,
            )
        p0 = new([P, O], F32, "p0")
        p1 = new([P, O], F32, "p1")
        nc.vector.tensor_copy(out=p0[:], in_=sums[0][:, 0:O])
        nc.vector.tensor_copy(pages[0][:].indirect(idx4[:]), p0[:])
        nc.sync.dma_start(out=out[0:P, :], in_=pages[0][:])
        nc.scalar.copy(out=p1[:], in_=sums[1][:, 0:O])
        nc.scalar.activation(out=pages[1][:].indirect(idx4[:]), in_=p1[:], func=ACT.Copy)
        nc.scalar.dma_start(out=out[P : 2 * P, :], in_=pages[1][:])
